import numpy as np
CORES = [2,10,18,26,34,42,50,58,66,74,82,90,98,106,114,122,130,138,146,154,162,170,178,186,194,202,210,218,226,234,242,250,258,266,274,282,290,298,306,314,322,330,338,346,354,362,370,378,386,394,402,410,418,426,434,442,450,458,466,474,482,490,498,506]
N = 64
def setup_inputs(rng):
    return {"x": rng.standard_normal((N, 128, 256), dtype=np.float32)}
def reference(x):
    s = x.sum(axis=0, dtype=np.float64).astype(x.dtype)
    return {"y": np.broadcast_to(s, (N,) + s.shape)}

@@ -1,0 +1,102 @@
+from concourse.bass import DstId, RemoteDMATransfer
+
+SCRATCH = {
+    "xs": ("sbuf", [128, 256], "float32"),
+    "ys": ("sbuf", [128, 256], "float32"),
+    "w1": ("sbuf", [128, 256], "float32"),
+    "w2": ("sbuf", [128, 128], "float32"),
+    "x3": ("sbuf", [128, 16], "float32"),
+    "y4": ("sbuf", [128, 16], "float32"),
+    "z": ("sbuf", [128, 128], "float32"),
+}
+SEMAPHORES = ["ld", "sent", "a1", "a2", "a3", "a4", "a5", "a6", "a7"]
+
+RANK, W, X, Y, Z = 2, 3, 1, 4, 6
+ADD = 1
+OFF = 0x00FF
+ON = 0xFF00
+
+
+def rank_program(g, core, T, topo):
+    role = core % 8
+    h, k = topo.host(core), topo.chip(core)
+    q, j = k % 2, k // 2
+    u = 0 if h in (0, 3) else 1
+    r = topo.rack(h)
+    S = T.sem
+
+    def at(hh, kk, c):
+        return hh * 128 + kk * 8 + c
+
+    def did(dst):
+        rid, pid = topo.addr(dst, core)
+        return DstId(rid=rid, pnc=pid)
+
+    peers = [s for s in range(8) if s != j]
+
+    if role == RANK:
+        g.dma_start(T.xs[:], T.x[:]).then_inc(S.ld, 16)
+        g.wait_ge(S.ld, 16)
+        g.remote_dma_fused([
+            RemoteDMATransfer(dst_ids=[did(at(h, k, W))], dma_engine_mask=ON, remote_sem=S.a1,
+                              src=T.xs[:, q * 128:(q + 1) * 128], dst=T.w1[:, q * 128:(q + 1) * 128]),
+            RemoteDMATransfer(dst_ids=[did(at(h, k ^ 1, W))], dma_engine_mask=OFF, remote_sem=S.a1,
+                              src=T.xs[:, (1 - q) * 128:(2 - q) * 128], dst=T.w1[:, q * 128:(q + 1) * 128]),
+        ], local_sem=S.sent)
+        g.wait_ge(S.a7, 16)
+        g.dma_start(T.y[:], T.ys[:]).then_inc(S.ld, 16)
+        g.wait_ge(S.ld, 32)
+        g.wait_ge(S.sent, 16)
+
+    elif role == W:
+        g.wait_ge(S.a1, 16)
+        g.remote_dma_fused([
+            RemoteDMATransfer(dst_ids=[did(at(h, 2 * s + q, W))], dma_engine_mask=1 << i, remote_sem=S.a2,
+                              srcs=[T.w1[:, s * 16:(s + 1) * 16], T.w1[:, 128 + s * 16:128 + (s + 1) * 16]],
+                              dsts=[T.w2[:, j * 16:(j + 1) * 16]], alu_op=ADD)
+            for i, s in enumerate(peers)], local_sem=S.sent)
+        g.wait_ge(S.a2, 7)
+        tr = []
+        for v in range(2):
+            o = j * 16 + v * 8
+            srcs = [T.w1[:, o:o + 8], T.w1[:, 128 + o:128 + o + 8]]
+            srcs += [T.w2[:, s * 16 + v * 8:s * 16 + v * 8 + 8] for s in peers]
+            hh = h if v == u else h ^ 1
+            tr.append(RemoteDMATransfer(dst_ids=[did(at(hh, k, X))], dma_engine_mask=ON if v == u else OFF,
+                                        remote_sem=S.a3, srcs=srcs, dsts=[T.x3[:, u * 8:u * 8 + 8]], alu_op=ADD))
+        g.remote_dma_fused(tr, local_sem=S.sent)
+        g.wait_ge(S.sent, 7 + 16)
+
+    elif role == X:
+        g.wait_ge(S.a3, 16)
+        g.remote_dma_fused([
+            RemoteDMATransfer(dst_ids=[did(at(h, k, Y)), did(at(3 - h, k, Y))], dma_engine_mask=OFF, remote_sem=S.a4,
+                              srcs=[T.x3[:, 0:8], T.x3[:, 8:16]],
+                              dsts=[T.y4[:, r * 8:r * 8 + 8], T.y4[:, r * 8:r * 8 + 8]], alu_op=ADD),
+        ], local_sem=S.sent)
+        g.wait_ge(S.sent, 8)
+
+    elif role == Y:
+        g.wait_ge(S.a4, 16)
+        o = j * 16 + u * 8
+        g.remote_dma_fused([
+            RemoteDMATransfer(dst_ids=[did(at(h, k, Z)), did(at(h ^ 1, k, Z))], dma_engine_mask=OFF, remote_sem=S.a5,
+                              srcs=[T.y4[:, 0:8], T.y4[:, 8:16]],
+                              dsts=[T.z[:, o:o + 8], T.z[:, o:o + 8]], alu_op=ADD),
+        ], local_sem=S.sent)
+        g.wait_ge(S.sent, 8)
+
+    elif role == Z:
+        g.wait_ge(S.a5, 16)
+        p = T.z[:, j * 16:(j + 1) * 16]
+        g.remote_dma_fused([
+            RemoteDMATransfer(dst_ids=[did(at(h, 2 * s + q, Z)) for s in peers], dma_engine_mask=OFF, remote_sem=S.a6,
+                              srcs=[p], dsts=[p for s in peers]),
+        ], local_sem=S.sent)
+        g.wait_ge(S.a6, 56)
+        d = T.ys[:, q * 128:(q + 1) * 128]
+        g.remote_dma_fused([
+            RemoteDMATransfer(dst_ids=[did(at(h, k, RANK)), did(at(h, k ^ 1, RANK))], dma_engine_mask=OFF,
+                              remote_sem=S.a7, srcs=[T.z[:]], dsts=[d, d]),
+        ], local_sem=S.sent)
+        g.wait_ge(S.sent, 16)

@@ -1,20 +1,17 @@
 from concourse.bass import DstId, RemoteDMATransfer
 
 SCRATCH = {
-    "xs": ("sbuf", [128, 256], "float32"),
-    "ys": ("sbuf", [128, 256], "float32"),
-    "w1": ("sbuf", [128, 256], "float32"),
-    "w2": ("sbuf", [128, 128], "float32"),
-    "x3": ("sbuf", [128, 16], "float32"),
-    "y4": ("sbuf", [128, 16], "float32"),
-    "z": ("sbuf", [128, 128], "float32"),
+    "xs": ("dram", [4, 128, 64], "float32"),
+    "ys": ("dram", [4, 128, 64], "float32"),
+    "pc": ("dram", [24, 128, 8], "float32"),
+    "x3": ("dram", [2, 128, 8], "float32"),
+    "y4": ("dram", [2, 128, 8], "float32"),
 }
 SEMAPHORES = ["ld", "sent", "a1", "a2", "a3", "a4", "a5", "a6", "a7"]
 
-RANK, W, X, Y, Z = 2, 3, 1, 4, 6
+RANK, WS, X, Y, ZS = 2, (0, 1), 3, 4, (6, 7)
 ADD = 1
 OFF = 0x00FF
-ON = 0xFF00
 
 
 def rank_program(g, core, T, topo):
@@ -24,79 +21,69 @@ def rank_program(g, core, T, topo):
     u = 0 if h in (0, 3) else 1
     r = topo.rack(h)
     S = T.sem
-
-    def at(hh, kk, c):
-        return hh * 128 + kk * 8 + c
-
-    def did(dst):
-        rid, pid = topo.addr(dst, core)
-        return DstId(rid=rid, pnc=pid)
-
     peers = [s for s in range(8) if s != j]
+
+    def did(hh, kk, c):
+        rid, pid = topo.addr(hh * 128 + kk * 8 + c, core)
+        return DstId(rid=rid, pnc=pid)
 
     if role == RANK:
         g.dma_start(T.xs[:], T.x[:]).then_inc(S.ld, 16)
         g.wait_ge(S.ld, 16)
         g.remote_dma_fused([
-            RemoteDMATransfer(dst_ids=[did(at(h, k, W))], dma_engine_mask=ON, remote_sem=S.a1,
-                              src=T.xs[:, q * 128:(q + 1) * 128], dst=T.w1[:, q * 128:(q + 1) * 128]),
-            RemoteDMATransfer(dst_ids=[did(at(h, k ^ 1, W))], dma_engine_mask=OFF, remote_sem=S.a1,
-                              src=T.xs[:, (1 - q) * 128:(2 - q) * 128], dst=T.w1[:, q * 128:(q + 1) * 128]),
-        ], local_sem=S.sent)
-        g.wait_ge(S.a7, 16)
+            RemoteDMATransfer(dst_ids=[did(h, k if p == q else k ^ 1, WS[v])],
+                              dma_engine_mask=0xF << (4 * v + (8 if p == q else 0)),
+                              remote_sem=S.a1, src=T.xs[2 * p + v], dst=T.xs[q])
+            for p in range(2) for v in range(2)], local_sem=S.sent)
+        g.wait_ge(S.a7, 32)
         g.dma_start(T.y[:], T.ys[:]).then_inc(S.ld, 16)
         g.wait_ge(S.ld, 32)
         g.wait_ge(S.sent, 16)
 
-    elif role == W:
-        g.wait_ge(S.a1, 16)
+    elif role in WS:
+        v = WS.index(role)
+        g.wait_ge(S.a1, 8)
+        g.dma_start(T.pc[0:16], T.xs[0:2]).then_inc(S.ld, 16)
+        g.wait_ge(S.ld, 16)
         g.remote_dma_fused([
-            RemoteDMATransfer(dst_ids=[did(at(h, 2 * s + q, W))], dma_engine_mask=1 << i, remote_sem=S.a2,
-                              srcs=[T.w1[:, s * 16:(s + 1) * 16], T.w1[:, 128 + s * 16:128 + (s + 1) * 16]],
-                              dsts=[T.w2[:, j * 16:(j + 1) * 16]], alu_op=ADD)
+            RemoteDMATransfer(dst_ids=[did(h, 2 * s + q, role)], dma_engine_mask=1 << i, remote_sem=S.a2,
+                              srcs=[T.pc[s], T.pc[8 + s]], dsts=[T.pc[16 + j]], alu_op=ADD)
             for i, s in enumerate(peers)], local_sem=S.sent)
         g.wait_ge(S.a2, 7)
-        tr = []
-        for v in range(2):
-            o = j * 16 + v * 8
-            srcs = [T.w1[:, o:o + 8], T.w1[:, 128 + o:128 + o + 8]]
-            srcs += [T.w2[:, s * 16 + v * 8:s * 16 + v * 8 + 8] for s in peers]
-            hh = h if v == u else h ^ 1
-            tr.append(RemoteDMATransfer(dst_ids=[did(at(hh, k, X))], dma_engine_mask=ON if v == u else OFF,
-                                        remote_sem=S.a3, srcs=srcs, dsts=[T.x3[:, u * 8:u * 8 + 8]], alu_op=ADD))
-        g.remote_dma_fused(tr, local_sem=S.sent)
-        g.wait_ge(S.sent, 7 + 16)
+        g.remote_dma_fused([
+            RemoteDMATransfer(dst_ids=[did(h if u == v else h ^ 1, k, X)], dma_engine_mask=OFF, remote_sem=S.a3,
+                              srcs=[T.pc[j], T.pc[8 + j]] + [T.pc[16 + s] for s in peers], dsts=[T.x3[u]], alu_op=ADD),
+        ], local_sem=S.sent)
+        g.wait_ge(S.sent, 7 + 8)
 
     elif role == X:
         g.wait_ge(S.a3, 16)
         g.remote_dma_fused([
-            RemoteDMATransfer(dst_ids=[did(at(h, k, Y)), did(at(3 - h, k, Y))], dma_engine_mask=OFF, remote_sem=S.a4,
-                              srcs=[T.x3[:, 0:8], T.x3[:, 8:16]],
-                              dsts=[T.y4[:, r * 8:r * 8 + 8], T.y4[:, r * 8:r * 8 + 8]], alu_op=ADD),
+            RemoteDMATransfer(dst_ids=[did(h, k, Y), did(3 - h, k, Y)], dma_engine_mask=OFF, remote_sem=S.a4,
+                              srcs=[T.x3[0], T.x3[1]], dsts=[T.y4[r], T.y4[r]], alu_op=ADD),
         ], local_sem=S.sent)
         g.wait_ge(S.sent, 8)
 
     elif role == Y:
         g.wait_ge(S.a4, 16)
-        o = j * 16 + u * 8
         g.remote_dma_fused([
-            RemoteDMATransfer(dst_ids=[did(at(h, k, Z)), did(at(h ^ 1, k, Z))], dma_engine_mask=OFF, remote_sem=S.a5,
-                              srcs=[T.y4[:, 0:8], T.y4[:, 8:16]],
-                              dsts=[T.z[:, o:o + 8], T.z[:, o:o + 8]], alu_op=ADD),
+            RemoteDMATransfer(dst_ids=[did(h, k, ZS[u]), did(h ^ 1, k, ZS[u])], dma_engine_mask=OFF, remote_sem=S.a5,
+                              srcs=[T.y4[0], T.y4[1]], dsts=[T.pc[j], T.pc[j]], alu_op=ADD),
         ], local_sem=S.sent)
         g.wait_ge(S.sent, 8)
 
-    elif role == Z:
-        g.wait_ge(S.a5, 16)
-        p = T.z[:, j * 16:(j + 1) * 16]
+    elif role in ZS:
+        v = ZS.index(role)
+        g.wait_ge(S.a5, 8)
         g.remote_dma_fused([
-            RemoteDMATransfer(dst_ids=[did(at(h, 2 * s + q, Z)) for s in peers], dma_engine_mask=OFF, remote_sem=S.a6,
-                              srcs=[p], dsts=[p for s in peers]),
+            RemoteDMATransfer(dst_ids=[did(h, 2 * s + q, role) for s in peers], dma_engine_mask=OFF, remote_sem=S.a6,
+                              srcs=[T.pc[j]], dsts=[T.pc[j] for s in peers]),
         ], local_sem=S.sent)
         g.wait_ge(S.a6, 56)
-        d = T.ys[:, q * 128:(q + 1) * 128]
+        g.dma_start(T.xs[0], T.pc[0:8]).then_inc(S.ld, 16)
+        g.wait_ge(S.ld, 16)
         g.remote_dma_fused([
-            RemoteDMATransfer(dst_ids=[did(at(h, k, RANK)), did(at(h, k ^ 1, RANK))], dma_engine_mask=OFF,
-                              remote_sem=S.a7, srcs=[T.z[:]], dsts=[d, d]),
+            RemoteDMATransfer(dst_ids=[did(h, k, RANK), did(h, k ^ 1, RANK)], dma_engine_mask=OFF, remote_sem=S.a7,
+                              srcs=[T.xs[0]], dsts=[T.ys[2 * q + v], T.ys[2 * q + v]]),
         ], local_sem=S.sent)
         g.wait_ge(S.sent, 16)

from concourse.bass import DstId, RemoteDMATransfer

SCRATCH = {
    "xs": ("dram", [4, 128, 64], "float32"),
    "ys": ("dram", [4, 128, 64], "float32"),
    "pc": ("dram", [24, 128, 8], "float32"),
    "x3": ("dram", [2, 128, 8], "float32"),
    "y4": ("dram", [2, 128, 8], "float32"),
}
SEMAPHORES = ["ld", "sent", "a1", "a2", "a3", "a4", "a5", "a6", "a7"]

RANK, WS, X, Y, ZS = 2, (0, 1), 3, 4, (6, 7)
ADD = 1
OFF = 0x00FF


def rank_program(g, core, T, topo):
    role = core % 8
    h, k = topo.host(core), topo.chip(core)
    q, j = k % 2, k // 2
    u = 0 if h in (0, 3) else 1
    r = topo.rack(h)
    S = T.sem
    peers = [s for s in range(8) if s != j]

    def did(hh, kk, c):
        rid, pid = topo.addr(hh * 128 + kk * 8 + c, core)
        return DstId(rid=rid, pnc=pid)

    if role == RANK:
        g.dma_start(T.xs[:], T.x[:]).then_inc(S.ld, 16)
        g.wait_ge(S.ld, 16)
        g.remote_dma_fused([
            RemoteDMATransfer(dst_ids=[did(h, k if p == q else k ^ 1, WS[v])],
                              dma_engine_mask=0xF << (4 * v + (8 if p == q else 0)),
                              remote_sem=S.a1, src=T.xs[2 * p + v], dst=T.xs[q])
            for p in range(2) for v in range(2)], local_sem=S.sent)
        g.wait_ge(S.a7, 32)
        g.dma_start(T.y[:], T.ys[:]).then_inc(S.ld, 16)
        g.wait_ge(S.ld, 32)
        g.wait_ge(S.sent, 16)

    elif role in WS:
        v = WS.index(role)
        g.wait_ge(S.a1, 8)
        g.dma_start(T.pc[0:16], T.xs[0:2]).then_inc(S.ld, 16)
        g.wait_ge(S.ld, 16)
        g.remote_dma_fused([
            RemoteDMATransfer(dst_ids=[did(h, 2 * s + q, role)], dma_engine_mask=1 << i, remote_sem=S.a2,
                              srcs=[T.pc[s], T.pc[8 + s]], dsts=[T.pc[16 + j]], alu_op=ADD)
            for i, s in enumerate(peers)], local_sem=S.sent)
        g.wait_ge(S.a2, 7)
        g.remote_dma_fused([
            RemoteDMATransfer(dst_ids=[did(h if u == v else h ^ 1, k, X)], dma_engine_mask=OFF, remote_sem=S.a3,
                              srcs=[T.pc[j], T.pc[8 + j]] + [T.pc[16 + s] for s in peers], dsts=[T.x3[u]], alu_op=ADD),
        ], local_sem=S.sent)
        g.wait_ge(S.sent, 7 + 8)

    elif role == X:
        g.wait_ge(S.a3, 16)
        g.remote_dma_fused([
            RemoteDMATransfer(dst_ids=[did(h, k, Y), did(3 - h, k, Y)], dma_engine_mask=OFF, remote_sem=S.a4,
                              srcs=[T.x3[0], T.x3[1]], dsts=[T.y4[r], T.y4[r]], alu_op=ADD),
        ], local_sem=S.sent)
        g.wait_ge(S.sent, 8)

    elif role == Y:
        g.wait_ge(S.a4, 16)
        g.remote_dma_fused([
            RemoteDMATransfer(dst_ids=[did(h, k, ZS[u]), did(h ^ 1, k, ZS[u])], dma_engine_mask=OFF, remote_sem=S.a5,
                              srcs=[T.y4[0], T.y4[1]], dsts=[T.pc[j], T.pc[j]], alu_op=ADD),
        ], local_sem=S.sent)
        g.wait_ge(S.sent, 8)

    elif role in ZS:
        v = ZS.index(role)
        g.wait_ge(S.a5, 8)
        g.remote_dma_fused([
            RemoteDMATransfer(dst_ids=[did(h, 2 * s + q, role) for s in peers], dma_engine_mask=OFF, remote_sem=S.a6,
                              srcs=[T.pc[j]], dsts=[T.pc[j] for s in peers]),
        ], local_sem=S.sent)
        g.wait_ge(S.a6, 56)
        g.dma_start(T.xs[0], T.pc[0:8]).then_inc(S.ld, 16)
        g.wait_ge(S.ld, 16)
        g.remote_dma_fused([
            RemoteDMATransfer(dst_ids=[did(h, k, RANK), did(h, k ^ 1, RANK)], dma_engine_mask=OFF, remote_sem=S.a7,
                              srcs=[T.xs[0]], dsts=[T.ys[2 * q + v], T.ys[2 * q + v]]),
        ], local_sem=S.sent)
        g.wait_ge(S.sent, 16)
